import numpy as np
import ml_dtypes


def mxq(x, axis, fmt="e4m3"):
    dtype, down = {"e4m3": (ml_dtypes.float8_e4m3fn, 7), "e5m2": (ml_dtypes.float8_e5m2, 14)}[fmt]
    v = np.moveaxis(np.asarray(x, np.float32).astype(ml_dtypes.bfloat16).astype(np.float64), axis, -1)
    blocks = v.reshape(v.shape[:-1] + (-1, 32))
    amax = np.abs(blocks).max(-1, keepdims=True)
    byte = np.maximum(np.where(amax > 0, np.frexp(amax)[1] - 1 + 127, 0) - down, 1)
    scale = np.exp2(byte - 127.0)
    codes = (blocks / scale).astype(np.float32).astype(dtype).astype(np.float64)
    return np.moveaxis((codes * scale).reshape(v.shape), -1, axis)


WIDE = False


def mx_kscale(k):
    if not WIDE:
        return np.ones(k)
    levels = np.array([10, -10, 5, -5, 0])
    if k % 512:
        return np.exp2(np.random.permutation(np.resize(levels, k // 32))).repeat(32)
    a = np.empty((k // 512, 16))
    for p in range(k // 512):
        a[p, :8] = np.random.permutation(np.resize(levels, 8))
        for g in range(8):
            far = levels[np.abs(levels - a[p, g]) >= 10]
            a[p, g + 8] = far[np.random.randint(len(far))]
    return np.exp2(a.ravel()).repeat(32)


def f64(x):
    return np.asarray(x).astype(np.float64)


def striped(idx):
    return np.tile(idx.reshape(-1, 16).T, (8, 1)).astype(np.uint16)


def unstriped(offs):
    return offs[:16].T.reshape(-1).astype(np.int64)


def striped8(idx):
    return np.concatenate([x.reshape(-1, 16).T for x in idx]).astype(np.uint16)


def runs(offs, k):
    lists = np.stack([offs[16 * r : 16 * r + 16].T.reshape(-1) for r in range(8)]).astype(np.int64)
    return lists[np.arange(k) % 512 // 64]


def pack_weight(w):
    k, n = w.shape
    w = f64(np.asarray(w, np.float32).astype(ml_dtypes.bfloat16)).reshape(k // 32, 32, n)
    amax = np.abs(w).max(1)
    byte = np.clip(np.where(amax > 0, np.frexp(amax)[1] - 1 + 127 - 7, 1), 1, 254)
    scaled = (w * np.exp2(127.0 - byte)[:, None, :]).reshape(k, n).astype(np.float32)
    words = np.ascontiguousarray(scaled.reshape(k // 512, 128, 4, n).transpose(0, 1, 3, 2)).astype(ml_dtypes.float8_e4m3fn).view(np.uint8)
    return words, np.ascontiguousarray(byte.astype(np.uint8).reshape(k // 512, 16, n))


def unpack_weight(words, scales):
    g, p, n, _ = words.shape
    vals = np.ascontiguousarray(words).view(ml_dtypes.float8_e4m3fn).astype(np.float64) * np.repeat(np.exp2(scales.astype(np.float64) - 127.0), 8, axis=1)[..., None]
    return vals.transpose(0, 1, 3, 2).reshape(g * 512, n)


E2M1 = np.array([0.0, 0.5, 1.0, 1.5, 2.0, 3.0, 4.0, 6.0, -0.0, -0.5, -1.0, -1.5, -2.0, -3.0, -4.0, -6.0])


def pack_fp4(w):
    k, n = w.shape
    w = f64(np.asarray(w, np.float32).astype(ml_dtypes.bfloat16)).reshape(k // 32, 32, n)
    amax = np.abs(w).max(1)
    mant, ex = np.frexp(amax / 6.0)
    byte = np.clip(np.where(amax > 0, np.where(mant > 0.5, ex, ex - 1) + 127, 1), 1, 254)
    scaled = (w * np.exp2(127.0 - byte)[:, None, :]).reshape(k, n).astype(np.float32)
    c = np.ascontiguousarray(scaled.reshape(k // 512, 128, 4, n).transpose(0, 1, 3, 2)).astype(ml_dtypes.float4_e2m1fn).view(np.uint8) & 0xF
    words = (c[..., 0::2] | (c[..., 1::2] << 4)).reshape(k // 512, 128, 2 * n)
    return np.ascontiguousarray(words), np.ascontiguousarray(byte.astype(np.uint8).reshape(k // 512, 16, n))


def unpack_fp4(words, scales):
    g, _, n = scales.shape
    words = np.ascontiguousarray(words).reshape(g, 128, n, 2)
    nib = np.empty((g, 128, n, 4), np.uint8)
    nib[..., 0::2] = words & 0xF
    nib[..., 1::2] = words >> 4
    vals = E2M1[nib] * np.repeat(np.exp2(scales.astype(np.float64) - 127.0), 8, axis=1)[..., None]
    return vals.transpose(0, 1, 3, 2).reshape(g * 512, n)


def planes(y):
    n, m = y.shape
    v = y.astype(np.float32).astype(ml_dtypes.bfloat16).astype(np.float64).reshape(n // 32, 32, m)
    top = np.abs(v).max(1)
    byte = np.clip(np.where(top > 0, np.frexp(top)[1] - 1 + 127 - 7, 1), 1, 254)
    codes = (v * np.exp2(127.0 - byte)[:, None, :]).reshape(n, m).astype(np.float32).astype(ml_dtypes.float8_e4m3fn).view(np.uint8)
    words = codes.reshape(n // 512, 128, 4, m).transpose(0, 1, 3, 2)
    return np.ascontiguousarray(words), np.ascontiguousarray(byte.astype(np.uint8).reshape(n // 512, 16, m))


K, T, S, H, G = 512, 2048, 512, 512, 2048


def setup_inputs():
    n = np.random.standard_normal
    s = mx_kscale(K)[:, None]
    packed_xT = pack_weight(n((K, T)) * s)
    packed_w1 = pack_fp4(n((K, H)) / np.sqrt(K) / s)
    packed_dT = pack_weight(n((K, G)) / s)
    return {
        "x_words": packed_xT[0],
        "x_scales": packed_xT[1],
        "w1_words": packed_w1[0],
        "w1_scales": packed_w1[1],
        "gs": (np.random.uniform(0.5, 1.5, (K, 1)) * s).astype(np.float32),
        "d_words": packed_dT[0],
        "d_scales": packed_dT[1],
        "offs": striped(np.random.permutation(T)[:S]),
        "n1": striped8(np.stack([np.random.permutation(S) for _ in range(8)])),
        "n2": striped8(np.stack([np.random.permutation(S) for _ in range(8)])),
        "k1": striped8(np.random.randint(0, G, (8, H))),
        "n3": striped8(np.stack([np.random.permutation(S) for _ in range(8)])),
        "n4": striped8(np.stack([np.random.permutation(S) for _ in range(8)])),
    }


def reference(x_words, x_scales, w1_words, w1_scales, gs, d_words, d_scales, offs, n1, n2, k1, n3, n4):
    d_k1 = unpack_weight(d_words, d_scales)[np.arange(K)[:, None], runs(k1, K)]
    xq = unpack_weight(x_words, x_scales)[:, unstriped(offs)]
    y = unpack_fp4(w1_words, w1_scales).T @ xq
    z = f64(gs) * (y[np.arange(H)[:, None], runs(n1, H)] - (y[np.arange(H)[:, None], runs(n2, H)]))
    h = 0.0625 * ((d_k1.T @ mxq(z, 0, "e4m3")))
    out_0 = h - (np.minimum(h[np.arange(H)[:, None], runs(n3, H)], h[np.arange(H)[:, None], runs(n4, H)]))
    return (out_0,) + planes(out_0)

@@ -1,0 +1,188 @@
+from contextlib import ExitStack
+
+import concourse.mybir as mybir
+
+F32 = mybir.dt.float32
+BF16 = mybir.dt.bfloat16
+I32 = mybir.dt.int32
+U32 = mybir.dt.uint32
+U16 = mybir.dt.uint16
+U8 = mybir.dt.uint8
+FP8X4 = mybir.dt.float8_e4m3fn_x4
+FP4X4 = mybir.dt.float4_e2m1fn_x4
+COPY = mybir.ActivationFunctionType.Copy
+SUBTRACT = mybir.AluOpType.subtract
+MINIMUM = mybir.AluOpType.min
+
+P = 128
+PACK = 4
+TABLE = 2048
+S = 512
+FLOPS = 2 * 2 * 512 * 512 * 512
+
+Z_SLICES = ((0, 256), (256, 384), (384, 512))
+OUT_SLICES = ((0, 256), (256, 384), (384, 512))
+
+
+def interleave(copy, dst, src):
+    copy(
+        out=dst[:].rearrange("p (c i) t -> p c t i", i=PACK),
+        in_=src[:].rearrange("p t (c i) -> p c t i", i=PACK),
+    )
+
+
+def tile_picked_densegapunder_none_po_kernel(
+    tc, x_words, x_scales, w1_words, w1_scales, gs, d_words, d_scales, offs, n1, n2, k1, n3, n4, out_0, out_1, out_2
+):
+    nc = tc.nc
+    with ExitStack() as ctx:
+        lists = ctx.enter_context(tc.tile_pool(name="lists", bufs=1))
+        sb = ctx.enter_context(tc.tile_pool(name="sb", bufs=1))
+        psum = ctx.enter_context(tc.psum_pool(name="psum", bufs=1))
+
+        def list_tile(name):
+            return lists.tile([P, S // 16], U16, name=name)
+
+        def tile(name, shape, dtype):
+            return sb.tile([P] + shape, dtype, name=name, align_bytes=64)
+
+        offs_t, k1_t = list_tile("offs_t"), list_tile("k1_t")
+        n1_t, n2_t, n3_t, n4_t = list_tile("n1_t"), list_tile("n2_t"), list_tile("n3_t"), list_tile("n4_t")
+
+        x_table = tile("x_table", [TABLE], I32)
+        d_table = tile("d_table", [TABLE], I32)
+        xs_table = tile("xs_table", [TABLE], U8)
+        ds_table = tile("ds_table", [TABLE], U8)
+        w1_raw = tile("w1_raw", [2 * S], U8)
+        w1s_raw = tile("w1s_raw", [S], U8)
+        gain = tile("gain", [PACK], F32)
+        d_plane = tile("d_plane", [S], U8)
+
+        nc.vector.memset(xs_table[:].bitcast(I32), 0)
+        nc.vector.memset(ds_table[:].bitcast(I32), 0)
+        nc.vector.memset(w1s_raw[:].bitcast(I32), 0)
+        nc.vector.memset(d_plane[:].bitcast(I32), 0)
+
+        nc.sync.dma_start(w1_raw[:].bitcast(I32), w1_words[0].bitcast(I32))
+        nc.sync.dma_start(offs_t[:], offs)
+        for q in range(4):
+            nc.sync.dma_start(xs_table[32 * q : 32 * q + 4, :].bitcast(I32), x_scales[0, 4 * q : 4 * q + 4, :].bitcast(I32))
+        nc.sync.dma_start(ds_table[0:P:8, :].bitcast(I32), d_scales[0].bitcast(I32))
+        nc.sync.dma_start(k1_t[:], k1)
+        for q in range(4):
+            nc.sync.dma_start(w1s_raw[32 * q : 32 * q + 4, :].bitcast(I32), w1_scales[0, 4 * q : 4 * q + 4, :].bitcast(I32))
+        nc.sync.dma_start(x_table[:], x_words[0].rearrange("p n t -> p (n t)").bitcast(I32))
+        nc.sync.dma_start(d_table[:], d_words[0].rearrange("p n t -> p (n t)").bitcast(I32))
+        nc.sync.dma_start(gain[:], gs.rearrange("(p t) o -> p (t o)", t=PACK))
+        nc.sync.dma_start(n2_t[:], n2)
+        nc.sync.dma_start(n1_t[:], n1)
+        nc.sync.dma_start(n3_t[:], n3)
+        nc.sync.dma_start(n4_t[:], n4)
+
+        w1_codes = tile("w1_codes", [2 * S], U8)
+        nc.vector.tensor_copy(
+            out=w1_codes[:].rearrange("p (t m b) -> p t m b", t=PACK, b=2),
+            in_=w1_raw[:].rearrange("p (m t b) -> p t m b", t=PACK, b=2),
+        )
+        x_plane = tile("x_plane", [S], U8)
+        nc.vector.tensor_copy(x_plane[:], xs_table[:].indirect(offs_t[:]))
+        ds_picked = tile("ds_picked", [S], U8)
+        nc.vector.tensor_copy(ds_picked[:], ds_table[:].indirect(k1_t[:]))
+        ds_dealt = tile("ds_dealt", [S], U8)
+        nc.vector.tensor_copy(
+            out=ds_dealt[:].rearrange("p (t m) -> p t m", t=PACK),
+            in_=ds_picked[:].rearrange("p (m t) -> p t m", t=PACK),
+        )
+        for q in range(4):
+            nc.sync.dma_start(d_plane[32 * q : 32 * q + 4, :].bitcast(I32), ds_dealt[32 * q : 32 * q + 32 : 8, :].bitcast(I32))
+        w1_plane = tile("w1_plane", [S], U8)
+        nc.vector.tensor_copy(
+            out=w1_plane[:].rearrange("p (t m) -> p t m", t=PACK),
+            in_=w1s_raw[:].rearrange("p (m t) -> p t m", t=PACK),
+        )
+        x_codes = tile("x_codes", [S], U32)
+        nc.vector.tensor_copy(x_codes[:], x_table[:].bitcast(U32).indirect(offs_t[:]))
+
+        y = []
+        for t in range(PACK):
+            y_bank = psum.tile([P, S], F32, name="y_bank%d" % t)
+            nc.tensor.matmul_mx(
+                out=y_bank[:],
+                lhsT=w1_codes[:, 2 * P * t : 2 * P * (t + 1)].bitcast(FP4X4),
+                lhsT_scale=w1_plane[:, P * t : P * (t + 1)],
+                rhs=x_codes[:].bitcast(FP8X4),
+                rhs_scale=x_plane[:],
+                start=True,
+                stop=True,
+            )
+            y_t = tile("y%d" % t, [S], F32)
+            nc.scalar.activation(out=y_t[:], in_=y_bank[:], func=COPY, scale=gain[:, t : t + 1])
+            y.append(y_t)
+
+        d_picked = tile("d_picked", [S], U32)
+        nc.vector.tensor_copy(d_picked[:], d_table[:].bitcast(U32).indirect(k1_t[:]))
+        d_codes = tile("d_codes", [S], I32)
+        nc.vector.tensor_copy(
+            out=d_codes[:].rearrange("p (t m) -> p m t", t=PACK),
+            in_=d_picked[:].bitcast(I32).rearrange("p (m t) -> p m t", t=PACK),
+        )
+
+        h_banks = [psum.tile([P, S], F32, name="h_bank%d" % t) for t in range(PACK)]
+        h = [tile("h%d" % t, [S], F32) for t in range(PACK)]
+        for lo, hi in Z_SLICES:
+            width = hi - lo
+            entries = slice(lo // 16, hi // 16)
+            y_n2 = tile("y_n2_%d" % lo, [PACK, width], F32)
+            z = tile("z_%d" % lo, [PACK, width], F32)
+            for t in range(PACK):
+                nc.vector.tensor_copy(y_n2[:, t, :], y[t][:].indirect(n2_t[:, entries]))
+            for t in range(PACK):
+                nc.vector.tensor_tensor(z[:, t, :], y[t][:].indirect(n1_t[:, entries]), y_n2[:, t, :], SUBTRACT)
+            z_rounded = tile("z_rounded_%d" % lo, [width, PACK], BF16)
+            interleave(nc.scalar.copy, z_rounded, z)
+            z_codes = tile("z_codes_%d" % lo, [width], U32)
+            z_plane = tile("z_plane_%d" % lo, [width], U8)
+            nc.vector.quantize_mx(
+                out=z_codes[:].bitcast(FP8X4), scales=z_plane[:], in_=z_rounded[:].rearrange("p c t -> p (c t)")
+            )
+            for t in range(PACK):
+                nc.tensor.matmul_mx(
+                    out=h_banks[t][:, lo:hi],
+                    lhsT=d_codes[:, P * t : P * (t + 1)].bitcast(FP8X4),
+                    lhsT_scale=d_plane[:, P * t : P * (t + 1)],
+                    rhs=z_codes[:].bitcast(FP8X4),
+                    rhs_scale=z_plane[:],
+                    start=True,
+                    stop=True,
+                )
+                nc.scalar.activation(out=h[t][:, lo:hi], in_=h_banks[t][:, lo:hi], func=COPY, scale=0.0625)
+
+        out_rows = out_0.rearrange("(p t) j -> p t j", t=PACK)
+        out_words = out_1[0].rearrange("p n t -> p (n t)").bitcast(I32)
+        out_codes = tile("out_codes", [S], I32)
+        out_plane = tile("out_plane", [S], U8)
+        for lo, hi in OUT_SLICES:
+            width = hi - lo
+            entries = slice(lo // 16, hi // 16)
+            h_n3 = tile("h_n3_%d" % lo, [PACK, width], F32)
+            h_n4 = tile("h_n4_%d" % lo, [PACK, width], F32)
+            for t in range(PACK):
+                nc.vector.tensor_copy(h_n3[:, t, :], h[t][:].indirect(n3_t[:, entries]))
+                nc.vector.tensor_copy(h_n4[:, t, :], h[t][:].indirect(n4_t[:, entries]))
+            least = tile("least_%d" % lo, [PACK, width], F32)
+            nc.vector.tensor_tensor(least[:], h_n3[:], h_n4[:], MINIMUM)
+            result = tile("result_%d" % lo, [PACK, width], F32)
+            for t in range(PACK):
+                nc.vector.tensor_tensor(result[:, t, :], h[t][:, lo:hi], least[:, t, :], SUBTRACT)
+            nc.sync.dma_start(out_rows[:, :, lo:hi], result[:])
+            rounded = tile("rounded_%d" % lo, [width, PACK], BF16)
+            interleave(nc.vector.tensor_copy if hi == S else nc.scalar.copy, rounded, result)
+            nc.vector.quantize_mx(
+                out=out_codes[:, lo:hi].bitcast(FP8X4),
+                scales=out_plane[:, lo:hi],
+                in_=rounded[:].rearrange("p c t -> p (c t)"),
+            )
+            nc.sync.dma_start(out_words[:, lo:hi], out_codes[:, lo:hi])
+        for q in range(4):
+            queue = nc.scalar if q % 2 else nc.sync
+            queue.dma_start(out_2[0, 4 * q : 4 * q + 4, :].bitcast(I32), out_plane[32 * q : 32 * q + 4, :].bitcast(I32))

@@ -20,8 +20,8 @@ TABLE = 2048
 S = 512
 FLOPS = 2 * 2 * 512 * 512 * 512
 
-Z_SLICES = ((0, 256), (256, 384), (384, 512))
-OUT_SLICES = ((0, 256), (256, 384), (384, 512))
+Z_SLICES = ((0, 256), (256, 512))
+OUT_SLICES = (((0, 256), ((0, 256),)), ((256, 512), ((256, 384), (384, 512))))
 
 
 def interleave(copy, dst, src):
@@ -44,7 +44,7 @@ def tile_picked_densegapunder_none_po_kernel(
             return lists.tile([P, S // 16], U16, name=name)
 
         def tile(name, shape, dtype):
-            return sb.tile([P] + shape, dtype, name=name, align_bytes=64)
+            return sb.tile([P] + shape, dtype, name=name, tag=name, align_bytes=64)
 
         offs_t, k1_t = list_tile("offs_t"), list_tile("k1_t")
         n1_t, n2_t, n3_t, n4_t = list_tile("n1_t"), list_tile("n2_t"), list_tile("n3_t"), list_tile("n4_t")
@@ -67,15 +67,15 @@ def tile_picked_densegapunder_none_po_kernel(
         nc.sync.dma_start(offs_t[:], offs)
         for q in range(4):
             nc.sync.dma_start(xs_table[32 * q : 32 * q + 4, :].bitcast(I32), x_scales[0, 4 * q : 4 * q + 4, :].bitcast(I32))
-        nc.sync.dma_start(ds_table[0:P:8, :].bitcast(I32), d_scales[0].bitcast(I32))
         nc.sync.dma_start(k1_t[:], k1)
+        nc.sync.dma_start(x_table[:], x_words[0].rearrange("p n t -> p (n t)").bitcast(I32))
         for q in range(4):
             nc.sync.dma_start(w1s_raw[32 * q : 32 * q + 4, :].bitcast(I32), w1_scales[0, 4 * q : 4 * q + 4, :].bitcast(I32))
-        nc.sync.dma_start(x_table[:], x_words[0].rearrange("p n t -> p (n t)").bitcast(I32))
-        nc.sync.dma_start(d_table[:], d_words[0].rearrange("p n t -> p (n t)").bitcast(I32))
+        nc.sync.dma_start(ds_table[0:P:8, :].bitcast(I32), d_scales[0].bitcast(I32))
         nc.sync.dma_start(gain[:], gs.rearrange("(p t) o -> p (t o)", t=PACK))
         nc.sync.dma_start(n2_t[:], n2)
         nc.sync.dma_start(n1_t[:], n1)
+        nc.sync.dma_start(d_table[:], d_words[0].rearrange("p n t -> p (n t)").bitcast(I32))
         nc.sync.dma_start(n3_t[:], n3)
         nc.sync.dma_start(n4_t[:], n4)
 
@@ -86,26 +86,17 @@ def tile_picked_densegapunder_none_po_kernel(
         )
         x_plane = tile("x_plane", [S], U8)
         nc.vector.tensor_copy(x_plane[:], xs_table[:].indirect(offs_t[:]))
-        ds_picked = tile("ds_picked", [S], U8)
-        nc.vector.tensor_copy(ds_picked[:], ds_table[:].indirect(k1_t[:]))
-        ds_dealt = tile("ds_dealt", [S], U8)
-        nc.vector.tensor_copy(
-            out=ds_dealt[:].rearrange("p (t m) -> p t m", t=PACK),
-            in_=ds_picked[:].rearrange("p (m t) -> p t m", t=PACK),
-        )
-        for q in range(4):
-            nc.sync.dma_start(d_plane[32 * q : 32 * q + 4, :].bitcast(I32), ds_dealt[32 * q : 32 * q + 32 : 8, :].bitcast(I32))
+        x_codes = tile("x_codes", [S], U32)
+        nc.vector.tensor_copy(x_codes[:], x_table[:].bitcast(U32).indirect(offs_t[:]))
         w1_plane = tile("w1_plane", [S], U8)
         nc.vector.tensor_copy(
             out=w1_plane[:].rearrange("p (t m) -> p t m", t=PACK),
             in_=w1s_raw[:].rearrange("p (m t) -> p t m", t=PACK),
         )
-        x_codes = tile("x_codes", [S], U32)
-        nc.vector.tensor_copy(x_codes[:], x_table[:].bitcast(U32).indirect(offs_t[:]))
 
         y = []
         for t in range(PACK):
-            y_bank = psum.tile([P, S], F32, name="y_bank%d" % t)
+            y_bank = psum.tile([P, S], F32, name="y_bank%d" % t, tag="y_bank%d" % t)
             nc.tensor.matmul_mx(
                 out=y_bank[:],
                 lhsT=w1_codes[:, 2 * P * t : 2 * P * (t + 1)].bitcast(FP4X4),
@@ -119,49 +110,78 @@ def tile_picked_densegapunder_none_po_kernel(
             nc.scalar.activation(out=y_t[:], in_=y_bank[:], func=COPY, scale=gain[:, t : t + 1])
             y.append(y_t)
 
-        d_picked = tile("d_picked", [S], U32)
-        nc.vector.tensor_copy(d_picked[:], d_table[:].bitcast(U32).indirect(k1_t[:]))
-        d_codes = tile("d_codes", [S], I32)
+        ds_picked = tile("ds_picked", [S], U8)
+        nc.vector.tensor_copy(ds_picked[:], ds_table[:].indirect(k1_t[:]))
+        ds_dealt = tile("ds_dealt", [S], U8)
         nc.vector.tensor_copy(
-            out=d_codes[:].rearrange("p (t m) -> p m t", t=PACK),
-            in_=d_picked[:].bitcast(I32).rearrange("p (m t) -> p m t", t=PACK),
+            out=ds_dealt[:].rearrange("p (t m) -> p t m", t=PACK),
+            in_=ds_picked[:].rearrange("p (m t) -> p t m", t=PACK),
         )
+        for q in range(4):
+            nc.sync.dma_start(d_plane[32 * q : 32 * q + 4, :].bitcast(I32), ds_dealt[32 * q : 32 * q + 32 : 8, :].bitcast(I32))
 
-        h_banks = [psum.tile([P, S], F32, name="h_bank%d" % t) for t in range(PACK)]
-        h = [tile("h%d" % t, [S], F32) for t in range(PACK)]
+        z_rounded = []
         for lo, hi in Z_SLICES:
             width = hi - lo
             entries = slice(lo // 16, hi // 16)
-            y_n2 = tile("y_n2_%d" % lo, [PACK, width], F32)
             z = tile("z_%d" % lo, [PACK, width], F32)
+            y_n2 = [tile("y_n2_%d_%d" % (lo, t), [width], F32) for t in range(PACK)]
             for t in range(PACK):
-                nc.vector.tensor_copy(y_n2[:, t, :], y[t][:].indirect(n2_t[:, entries]))
-            for t in range(PACK):
-                nc.vector.tensor_tensor(z[:, t, :], y[t][:].indirect(n1_t[:, entries]), y_n2[:, t, :], SUBTRACT)
-            z_rounded = tile("z_rounded_%d" % lo, [width, PACK], BF16)
-            interleave(nc.scalar.copy, z_rounded, z)
-            z_codes = tile("z_codes_%d" % lo, [width], U32)
-            z_plane = tile("z_plane_%d" % lo, [width], U8)
+                nc.vector.tensor_copy(y_n2[t][:], y[t][:].indirect(n2_t[:, entries]))
+                if hi == S and t == PACK - 1:
+                    nc.vector.tensor_tensor(z[:, t, :], y[t][:].indirect(n1_t[:, entries]), y_n2[t][:], SUBTRACT)
+                else:
+                    y_n1 = tile("y_n1_%d_%d" % (lo, t), [width], F32)
+                    nc.vector.tensor_copy(y_n1[:], y[t][:].indirect(n1_t[:, entries]))
+                    nc.gpsimd.tensor_tensor(z[:, t, :], y_n1[:], y_n2[t][:], SUBTRACT)
+            z_bf = tile("z_rounded_%d" % lo, [width, PACK], BF16)
+            interleave(nc.scalar.copy, z_bf, z)
+            z_rounded.append(z_bf)
+
+        d_picked = sb.tile([P, S], U32, name="d_picked", tag="y_n2_%d_%d" % (Z_SLICES[-1][0], PACK - 3), align_bytes=64)
+        nc.vector.tensor_copy(d_picked[:], d_table[:].bitcast(U32).indirect(k1_t[:]))
+        z_codes = tile("z_codes", [S], U32)
+        z_plane = tile("z_plane", [S], U8)
+        d_codes = tile("d_codes", [S], I32)
+        for (lo, hi), z_bf in zip(Z_SLICES, z_rounded):
+            if hi == S:
+                nc.vector.tensor_copy(
+                    out=d_codes[:].rearrange("p (t m) -> p m t", t=PACK),
+                    in_=d_picked[:].bitcast(I32).rearrange("p (m t) -> p m t", t=PACK),
+                )
             nc.vector.quantize_mx(
-                out=z_codes[:].bitcast(FP8X4), scales=z_plane[:], in_=z_rounded[:].rearrange("p c t -> p (c t)")
+                out=z_codes[:, lo:hi].bitcast(FP8X4), scales=z_plane[:, lo:hi], in_=z_bf[:].rearrange("p c t -> p (c t)")
             )
-            for t in range(PACK):
+
+        h_banks = []
+        h = []
+        for t in range(PACK):
+            h_t = tile("h%d" % t, [S], F32)
+            for lo, hi in Z_SLICES if t == 0 else ((0, S),):
+                tag = "y_bank0" if hi < S else "h_bank%d" % t
+                h_bank = psum.tile([P, S], F32, name="h_bank%d_%d" % (t, lo), tag=tag)
                 nc.tensor.matmul_mx(
-                    out=h_banks[t][:, lo:hi],
+                    out=h_bank[:, lo:hi],
                     lhsT=d_codes[:, P * t : P * (t + 1)].bitcast(FP8X4),
                     lhsT_scale=d_plane[:, P * t : P * (t + 1)],
-                    rhs=z_codes[:].bitcast(FP8X4),
-                    rhs_scale=z_plane[:],
+                    rhs=z_codes[:, lo:hi].bitcast(FP8X4),
+                    rhs_scale=z_plane[:, lo:hi],
                     start=True,
                     stop=True,
                 )
-                nc.scalar.activation(out=h[t][:, lo:hi], in_=h_banks[t][:, lo:hi], func=COPY, scale=0.0625)
+                nc.scalar.activation(out=h_t[:, lo:hi], in_=h_bank[:, lo:hi], func=COPY, scale=0.0625)
+                h_banks.append((t, lo, hi, h_bank))
+            h.append(h_t)
+        h_rows = tile("h_rows", [PACK, S], F32)
+        for t, lo, hi, h_bank in h_banks:
+            nc.scalar.activation(out=h_rows[:, t, lo:hi], in_=h_bank[:, lo:hi], func=COPY, scale=0.0625)
 
         out_rows = out_0.rearrange("(p t) j -> p t j", t=PACK)
         out_words = out_1[0].rearrange("p n t -> p (n t)").bitcast(I32)
         out_codes = tile("out_codes", [S], I32)
         out_plane = tile("out_plane", [S], U8)
-        for lo, hi in OUT_SLICES:
+        waiting = []
+        for (lo, hi), parts in OUT_SLICES:
             width = hi - lo
             entries = slice(lo // 16, hi // 16)
             h_n3 = tile("h_n3_%d" % lo, [PACK, width], F32)
@@ -169,20 +189,26 @@ def tile_picked_densegapunder_none_po_kernel(
             for t in range(PACK):
                 nc.vector.tensor_copy(h_n3[:, t, :], h[t][:].indirect(n3_t[:, entries]))
                 nc.vector.tensor_copy(h_n4[:, t, :], h[t][:].indirect(n4_t[:, entries]))
-            least = tile("least_%d" % lo, [PACK, width], F32)
-            nc.vector.tensor_tensor(least[:], h_n3[:], h_n4[:], MINIMUM)
-            result = tile("result_%d" % lo, [PACK, width], F32)
-            for t in range(PACK):
-                nc.vector.tensor_tensor(result[:, t, :], h[t][:, lo:hi], least[:, t, :], SUBTRACT)
-            nc.sync.dma_start(out_rows[:, :, lo:hi], result[:])
-            rounded = tile("rounded_%d" % lo, [width, PACK], BF16)
-            interleave(nc.vector.tensor_copy if hi == S else nc.scalar.copy, rounded, result)
+            leasts = []
+            for a, b in parts:
+                least = tile("least_%d" % a, [PACK, b - a], F32)
+                nc.vector.tensor_tensor(least[:], h_n3[:, :, a - lo : b - lo], h_n4[:, :, a - lo : b - lo], MINIMUM)
+                leasts.append(least)
+            for (a, b), least in zip(parts, leasts):
+                result = tile("result_%d" % a, [PACK, b - a], F32)
+                engine = nc.gpsimd if a == 0 else nc.vector
+                engine.tensor_tensor(result[:], h_rows[:, :, a:b], least[:], SUBTRACT)
+                nc.sync.dma_start(out_rows[:, :, a:b], result[:])
+                rounded = tile("rounded_%d" % a, [b - a, PACK], BF16)
+                interleave(nc.vector.tensor_copy if b == S else nc.scalar.copy, rounded, result)
+                waiting.append((a, b, rounded))
+        for a, b, rounded in waiting:
             nc.vector.quantize_mx(
-                out=out_codes[:, lo:hi].bitcast(FP8X4),
-                scales=out_plane[:, lo:hi],
+                out=out_codes[:, a:b].bitcast(FP8X4),
+                scales=out_plane[:, a:b],
                 in_=rounded[:].rearrange("p c t -> p (c t)"),
             )
-            nc.sync.dma_start(out_words[:, lo:hi], out_codes[:, lo:hi])
+            nc.scalar.dma_start(out_words[:, a:b], out_codes[:, a:b])
         for q in range(4):
             queue = nc.scalar if q % 2 else nc.sync
             queue.dma_start(out_2[0, 4 * q : 4 * q + 4, :].bitcast(I32), out_plane[32 * q : 32 * q + 4, :].bitcast(I32))

@@ -12,7 +12,8 @@ FP8X4 = mybir.dt.float8_e4m3fn_x4
 FP4X4 = mybir.dt.float4_e2m1fn_x4
 COPY = mybir.ActivationFunctionType.Copy
 SUBTRACT = mybir.AluOpType.subtract
-MINIMUM = mybir.AluOpType.min
+ADD = mybir.AluOpType.add
+MAXIMUM = mybir.AluOpType.max
 
 P = 128
 PACK = 4
@@ -20,14 +21,14 @@ TABLE = 2048
 S = 512
 FLOPS = 2 * 2 * 512 * 512 * 512
 
-Z_SLICES = ((0, 256), (256, 512))
-OUT_SLICES = (((0, 256), ((0, 256),)), ((256, 512), ((256, 384), (384, 512))))
+HALVES = ((0, 256), (256, 512))
+LAST_PARTS = ((0, 256), (256, 384), (384, 512))
 
 
 def interleave(copy, dst, src):
     copy(
-        out=dst[:].rearrange("p (c i) t -> p c t i", i=PACK),
-        in_=src[:].rearrange("p t (c i) -> p c t i", i=PACK),
+        out=dst.rearrange("p (c i) t -> p c t i", i=PACK),
+        in_=src.rearrange("p t (c i) -> p c t i", i=PACK),
     )
 
 
@@ -50,7 +51,6 @@ def tile_picked_densegapunder_none_po_kernel(
         n1_t, n2_t, n3_t, n4_t = list_tile("n1_t"), list_tile("n2_t"), list_tile("n3_t"), list_tile("n4_t")
 
         x_table = tile("x_table", [TABLE], I32)
-        d_table = tile("d_table", [TABLE], I32)
         xs_table = tile("xs_table", [TABLE], U8)
         ds_table = tile("ds_table", [TABLE], U8)
         w1_raw = tile("w1_raw", [2 * S], U8)
@@ -59,14 +59,15 @@ def tile_picked_densegapunder_none_po_kernel(
         d_plane = tile("d_plane", [S], U8)
 
         nc.vector.memset(xs_table[:].bitcast(I32), 0)
-        nc.vector.memset(ds_table[:].bitcast(I32), 0)
         nc.vector.memset(w1s_raw[:].bitcast(I32), 0)
+        nc.vector.memset(ds_table[:].bitcast(I32), 0)
         nc.vector.memset(d_plane[:].bitcast(I32), 0)
 
+        queues = (nc.sync, nc.scalar)
         nc.sync.dma_start(w1_raw[:].bitcast(I32), w1_words[0].bitcast(I32))
         nc.sync.dma_start(offs_t[:], offs)
         for q in range(4):
-            nc.sync.dma_start(xs_table[32 * q : 32 * q + 4, :].bitcast(I32), x_scales[0, 4 * q : 4 * q + 4, :].bitcast(I32))
+            queues[q % 2].dma_start(xs_table[32 * q : 32 * q + 4, :].bitcast(I32), x_scales[0, 4 * q : 4 * q + 4, :].bitcast(I32))
         nc.sync.dma_start(k1_t[:], k1)
         nc.sync.dma_start(x_table[:], x_words[0].rearrange("p n t -> p (n t)").bitcast(I32))
         for q in range(4):
@@ -75,7 +76,6 @@ def tile_picked_densegapunder_none_po_kernel(
         nc.sync.dma_start(gain[:], gs.rearrange("(p t) o -> p (t o)", t=PACK))
         nc.sync.dma_start(n2_t[:], n2)
         nc.sync.dma_start(n1_t[:], n1)
-        nc.sync.dma_start(d_table[:], d_words[0].rearrange("p n t -> p (n t)").bitcast(I32))
         nc.sync.dma_start(n3_t[:], n3)
         nc.sync.dma_start(n4_t[:], n4)
 
@@ -84,6 +84,8 @@ def tile_picked_densegapunder_none_po_kernel(
             out=w1_codes[:].rearrange("p (t m b) -> p t m b", t=PACK, b=2),
             in_=w1_raw[:].rearrange("p (m t b) -> p t m b", t=PACK, b=2),
         )
+        d_table = sb.tile([P, TABLE], I32, name="d_table", tag="w1_raw", align_bytes=64)
+        nc.sync.dma_start(d_table[:], d_words[0].rearrange("p n t -> p (n t)").bitcast(I32))
         x_plane = tile("x_plane", [S], U8)
         nc.vector.tensor_copy(x_plane[:], xs_table[:].indirect(offs_t[:]))
         x_codes = tile("x_codes", [S], U32)
@@ -120,30 +122,34 @@ def tile_picked_densegapunder_none_po_kernel(
         for q in range(4):
             nc.sync.dma_start(d_plane[32 * q : 32 * q + 4, :].bitcast(I32), ds_dealt[32 * q : 32 * q + 32 : 8, :].bitcast(I32))
 
+        z = [tile("z_%d" % lo, [PACK, hi - lo], F32) for lo, hi in HALVES]
+
+        def difference(units):
+            picked = []
+            for t, half in units:
+                lo, hi = HALVES[half]
+                y_n2 = tile("y_n2_%d_%d" % (t, half), [hi - lo], F32)
+                nc.vector.tensor_copy(y_n2[:], y[t][:].indirect(n2_t[:, lo // 16 : hi // 16]))
+                picked.append(y_n2)
+            for (t, half), y_n2 in zip(units, picked):
+                lo, hi = HALVES[half]
+                nc.vector.tensor_tensor(z[half][:, t, :], y[t][:].indirect(n1_t[:, lo // 16 : hi // 16]), y_n2[:], SUBTRACT)
+
+        difference(((0, 0), (0, 1)))
+        difference(((1, 0), (1, 1)))
         z_rounded = []
-        for lo, hi in Z_SLICES:
-            width = hi - lo
-            entries = slice(lo // 16, hi // 16)
-            z = tile("z_%d" % lo, [PACK, width], F32)
-            y_n2 = [tile("y_n2_%d_%d" % (lo, t), [width], F32) for t in range(PACK)]
-            for t in range(PACK):
-                nc.vector.tensor_copy(y_n2[t][:], y[t][:].indirect(n2_t[:, entries]))
-                if hi == S and t == PACK - 1:
-                    nc.vector.tensor_tensor(z[:, t, :], y[t][:].indirect(n1_t[:, entries]), y_n2[t][:], SUBTRACT)
-                else:
-                    y_n1 = tile("y_n1_%d_%d" % (lo, t), [width], F32)
-                    nc.vector.tensor_copy(y_n1[:], y[t][:].indirect(n1_t[:, entries]))
-                    nc.gpsimd.tensor_tensor(z[:, t, :], y_n1[:], y_n2[t][:], SUBTRACT)
-            z_bf = tile("z_rounded_%d" % lo, [width, PACK], BF16)
-            interleave(nc.scalar.copy, z_bf, z)
+        for half, (lo, hi) in enumerate(HALVES):
+            difference(((2, half), (3, half)))
+            z_bf = tile("z_rounded_%d" % lo, [hi - lo, PACK], BF16)
+            interleave(nc.scalar.copy, z_bf[:], z[half][:])
             z_rounded.append(z_bf)
 
-        d_picked = sb.tile([P, S], U32, name="d_picked", tag="y_n2_%d_%d" % (Z_SLICES[-1][0], PACK - 3), align_bytes=64)
+        d_picked = sb.tile([P, S], U32, name="d_picked", tag="y_n2_2_1", align_bytes=64)
         nc.vector.tensor_copy(d_picked[:], d_table[:].bitcast(U32).indirect(k1_t[:]))
         z_codes = tile("z_codes", [S], U32)
         z_plane = tile("z_plane", [S], U8)
         d_codes = tile("d_codes", [S], I32)
-        for (lo, hi), z_bf in zip(Z_SLICES, z_rounded):
+        for (lo, hi), z_bf in zip(HALVES, z_rounded):
             if hi == S:
                 nc.vector.tensor_copy(
                     out=d_codes[:].rearrange("p (t m) -> p m t", t=PACK),
@@ -153,11 +159,11 @@ def tile_picked_densegapunder_none_po_kernel(
                 out=z_codes[:, lo:hi].bitcast(FP8X4), scales=z_plane[:, lo:hi], in_=z_bf[:].rearrange("p c t -> p (c t)")
             )
 
-        h_banks = []
-        h = []
+        windows = [tile("window%d" % t, [2 * S if t in (1, 2) else S], F32) for t in range(PACK)]
+        h_2, h_3 = tile("h_2", [S], F32), tile("h_3", [S], F32)
+        h = [windows[1][:, S:], windows[2][:, S:], h_2[:], h_3[:]]
         for t in range(PACK):
-            h_t = tile("h%d" % t, [S], F32)
-            for lo, hi in Z_SLICES if t == 0 else ((0, S),):
+            for lo, hi in HALVES if t == 0 else ((0, S),):
                 tag = "y_bank0" if hi < S else "h_bank%d" % t
                 h_bank = psum.tile([P, S], F32, name="h_bank%d_%d" % (t, lo), tag=tag)
                 nc.tensor.matmul_mx(
@@ -169,46 +175,62 @@ def tile_picked_densegapunder_none_po_kernel(
                     start=True,
                     stop=True,
                 )
-                nc.scalar.activation(out=h_t[:, lo:hi], in_=h_bank[:, lo:hi], func=COPY, scale=0.0625)
-                h_banks.append((t, lo, hi, h_bank))
-            h.append(h_t)
-        h_rows = tile("h_rows", [PACK, S], F32)
-        for t, lo, hi, h_bank in h_banks:
-            nc.scalar.activation(out=h_rows[:, t, lo:hi], in_=h_bank[:, lo:hi], func=COPY, scale=0.0625)
+                nc.scalar.activation(out=windows[t][:, lo:hi], in_=h_bank[:, lo:hi], func=COPY, scale=-0.0625)
+                nc.scalar.activation(out=h[t][:, lo:hi], in_=h_bank[:, lo:hi], func=COPY, scale=0.0625)
 
         out_rows = out_0.rearrange("(p t) j -> p t j", t=PACK)
         out_words = out_1[0].rearrange("p n t -> p (n t)").bitcast(I32)
         out_codes = tile("out_codes", [S], I32)
         out_plane = tile("out_plane", [S], U8)
-        waiting = []
-        for (lo, hi), parts in OUT_SLICES:
-            width = hi - lo
-            entries = slice(lo // 16, hi // 16)
-            h_n3 = tile("h_n3_%d" % lo, [PACK, width], F32)
-            h_n4 = tile("h_n4_%d" % lo, [PACK, width], F32)
-            for t in range(PACK):
-                nc.vector.tensor_copy(h_n3[:, t, :], h[t][:].indirect(n3_t[:, entries]))
-                nc.vector.tensor_copy(h_n4[:, t, :], h[t][:].indirect(n4_t[:, entries]))
-            leasts = []
-            for a, b in parts:
-                least = tile("least_%d" % a, [PACK, b - a], F32)
-                nc.vector.tensor_tensor(least[:], h_n3[:, :, a - lo : b - lo], h_n4[:, :, a - lo : b - lo], MINIMUM)
-                leasts.append(least)
-            for (a, b), least in zip(parts, leasts):
-                result = tile("result_%d" % a, [PACK, b - a], F32)
-                engine = nc.gpsimd if a == 0 else nc.vector
-                engine.tensor_tensor(result[:], h_rows[:, :, a:b], least[:], SUBTRACT)
-                nc.sync.dma_start(out_rows[:, :, a:b], result[:])
-                rounded = tile("rounded_%d" % a, [b - a, PACK], BF16)
-                interleave(nc.vector.tensor_copy if b == S else nc.scalar.copy, rounded, result)
-                waiting.append((a, b, rounded))
-        for a, b, rounded in waiting:
+        gap3 = tile("gap3", [PACK, S], F32)
+        gap4 = tile("gap4", [PACK, S], F32)
+        result = tile("result", [PACK, S], F32)
+
+        def gap(dst, entries, t, lo, hi):
+            nc.vector.tensor_tensor(dst[:, t, lo:hi], windows[t][:].indirect(entries[:, lo // 16 : hi // 16]), h[t][:, lo:hi], ADD)
+
+        def larger(rows, lo, hi):
+            nc.vector.tensor_tensor(result[:, rows, lo:hi], gap3[:, rows, lo:hi], gap4[:, rows, lo:hi], MAXIMUM)
+            nc.sync.dma_start(out_rows[:, rows, lo:hi], result[:, rows, lo:hi])
+
+        def rounded(copy, lo, hi):
+            out_bf = tile("out_bf_%d" % lo, [hi - lo, PACK], BF16)
+            interleave(copy, out_bf[:], result[:, :, lo:hi])
+            return out_bf
+
+        def quantize(out_bf, lo, hi):
             nc.vector.quantize_mx(
-                out=out_codes[:, a:b].bitcast(FP8X4),
-                scales=out_plane[:, a:b],
-                in_=rounded[:].rearrange("p c t -> p (c t)"),
+                out=out_codes[:, lo:hi].bitcast(FP8X4),
+                scales=out_plane[:, lo:hi],
+                in_=out_bf[:].rearrange("p c t -> p (c t)"),
             )
-            nc.scalar.dma_start(out_words[:, a:b], out_codes[:, a:b])
+
+        for lo, hi in HALVES:
+            gap(gap3, n3_t, 0, lo, hi)
+            gap(gap4, n4_t, 0, lo, hi)
+        gap(gap3, n3_t, 1, 0, S)
+        gap(gap4, n4_t, 1, 0, S)
+        gap(gap3, n3_t, 2, 0, S)
+        larger(slice(0, 2), 0, S)
+        gap(gap4, n4_t, 2, 0, S)
+        (a0, a1), (b0, b1), (c0, c1) = LAST_PARTS
+        gap(gap3, n3_t, 3, a0, a1)
+        larger(slice(2, 3), 0, S)
+        gap(gap4, n4_t, 3, a0, a1)
+        gap(gap3, n3_t, 3, b0, b1)
+        larger(slice(3, 4), a0, a1)
+        out_a = rounded(nc.scalar.copy, a0, a1)
+        gap(gap4, n4_t, 3, b0, b1)
+        gap(gap3, n3_t, 3, c0, c1)
+        larger(slice(3, 4), b0, b1)
+        out_b = rounded(nc.scalar.copy, b0, b1)
+        gap(gap4, n4_t, 3, c0, c1)
+        quantize(out_a, a0, a1)
+        nc.sync.dma_start(out_words[:, a0:a1], out_codes[:, a0:a1])
+        larger(slice(3, 4), c0, c1)
+        out_c = rounded(nc.vector.tensor_copy, c0, c1)
+        quantize(out_b, b0, b1)
+        quantize(out_c, c0, c1)
+        nc.sync.dma_start(out_words[:, b0:c1], out_codes[:, b0:c1])
         for q in range(4):
-            queue = nc.scalar if q % 2 else nc.sync
-            queue.dma_start(out_2[0, 4 * q : 4 * q + 4, :].bitcast(I32), out_plane[32 * q : 32 * q + 4, :].bitcast(I32))
+            queues[1 - q % 2].dma_start(out_2[0, 4 * q : 4 * q + 4, :].bitcast(I32), out_plane[32 * q : 32 * q + 4, :].bitcast(I32))

@@ -1,6 +1,7 @@
 from contextlib import ExitStack
 
 import concourse.mybir as mybir
+from concourse.masks import make_identity
 
 F32 = mybir.dt.float32
 BF16 = mybir.dt.bfloat16
@@ -11,6 +12,8 @@ U8 = mybir.dt.uint8
 FP8X4 = mybir.dt.float8_e4m3fn_x4
 FP4X4 = mybir.dt.float4_e2m1fn_x4
 COPY = mybir.ActivationFunctionType.Copy
+RELU = mybir.ActivationFunctionType.Relu
+MULTIPLY = mybir.AluOpType.mult
 SUBTRACT = mybir.AluOpType.subtract
 ADD = mybir.AluOpType.add
 MAXIMUM = mybir.AluOpType.max
@@ -62,6 +65,9 @@ def tile_picked_densegapunder_none_po_kernel(
         nc.vector.memset(w1s_raw[:].bitcast(I32), 0)
         nc.vector.memset(ds_table[:].bitcast(I32), 0)
         nc.vector.memset(d_plane[:].bitcast(I32), 0)
+
+        identity = tile("identity", [P], F32)
+        make_identity(nc, identity[:])
 
         queues = (nc.sync, nc.scalar)
         nc.sync.dma_start(w1_raw[:].bitcast(I32), w1_words[0].bitcast(I32))
@@ -148,34 +154,37 @@ def tile_picked_densegapunder_none_po_kernel(
         nc.vector.tensor_copy(d_picked[:], d_table[:].bitcast(U32).indirect(k1_t[:]))
         z_codes = tile("z_codes", [S], U32)
         z_plane = tile("z_plane", [S], U8)
-        d_codes = tile("d_codes", [S], I32)
+        picked_by_row = d_picked[:].bitcast(I32).rearrange("p (m t) -> p m t", t=PACK)
+        d_first = tile("d_first", [P], I32)
         for (lo, hi), z_bf in zip(HALVES, z_rounded):
             if hi == S:
-                nc.vector.tensor_copy(
-                    out=d_codes[:].rearrange("p (t m) -> p m t", t=PACK),
-                    in_=d_picked[:].bitcast(I32).rearrange("p (m t) -> p m t", t=PACK),
-                )
+                nc.vector.tensor_copy(out=d_first[:], in_=picked_by_row[:, :, 0])
             nc.vector.quantize_mx(
                 out=z_codes[:, lo:hi].bitcast(FP8X4), scales=z_plane[:, lo:hi], in_=z_bf[:].rearrange("p c t -> p (c t)")
             )
 
-        windows = [tile("window%d" % t, [2 * S if t in (1, 2) else S], F32) for t in range(PACK)]
-        h_2, h_3 = tile("h_2", [S], F32), tile("h_3", [S], F32)
-        h = [windows[1][:, S:], windows[2][:, S:], h_2[:], h_3[:]]
+        d_rest = sb.tile([P, PACK - 1, P], I32, name="d_rest", tag="z_rounded_%d" % HALVES[1][0], align_bytes=64)
+        nc.vector.tensor_copy(out=d_rest[:].rearrange("p t m -> p m t"), in_=picked_by_row[:, :, 1:])
+        d_codes = [d_first[:]] + [d_rest[:, t, :] for t in range(PACK - 1)]
+
+        windows = [tile("window%d" % t, [2 * S if t == 2 else S], F32) for t in range(PACK)]
+        h_2 = tile("h_2", [S], F32)
+        h = [windows[0][:], windows[1][:], h_2[:], windows[2][:, S:]]
         for t in range(PACK):
             for lo, hi in HALVES if t == 0 else ((0, S),):
                 tag = "y_bank0" if hi < S else "h_bank%d" % t
                 h_bank = psum.tile([P, S], F32, name="h_bank%d_%d" % (t, lo), tag=tag)
                 nc.tensor.matmul_mx(
                     out=h_bank[:, lo:hi],
-                    lhsT=d_codes[:, P * t : P * (t + 1)].bitcast(FP8X4),
+                    lhsT=d_codes[t].bitcast(FP8X4),
                     lhsT_scale=d_plane[:, P * t : P * (t + 1)],
                     rhs=z_codes[:, lo:hi].bitcast(FP8X4),
                     rhs_scale=z_plane[:, lo:hi],
                     start=True,
                     stop=True,
                 )
-                nc.scalar.activation(out=windows[t][:, lo:hi], in_=h_bank[:, lo:hi], func=COPY, scale=-0.0625)
+                if t >= 2:
+                    nc.scalar.activation(out=windows[t][:, lo:hi], in_=h_bank[:, lo:hi], func=COPY, scale=-0.0625)
                 nc.scalar.activation(out=h[t][:, lo:hi], in_=h_bank[:, lo:hi], func=COPY, scale=0.0625)
 
         out_rows = out_0.rearrange("(p t) j -> p t j", t=PACK)
@@ -205,13 +214,32 @@ def tile_picked_densegapunder_none_po_kernel(
                 in_=out_bf[:].rearrange("p c t -> p (c t)"),
             )
 
-        for lo, hi in HALVES:
-            gap(gap3, n3_t, 0, lo, hi)
-            gap(gap4, n4_t, 0, lo, hi)
-        gap(gap3, n3_t, 1, 0, S)
-        gap(gap4, n4_t, 1, 0, S)
+        for t in (0, 1):
+            for lo, hi in HALVES:
+                nc.vector.tensor_scalar(
+                    gap3[:, t, lo:hi], windows[t][:].indirect(n3_t[:, lo // 16 : hi // 16]), -1.0, 0.0, MULTIPLY, ADD
+                )
+            for lo, hi in HALVES:
+                nc.vector.tensor_tensor(
+                    gap4[:, t, lo:hi], windows[t][:].indirect(n4_t[:, lo // 16 : hi // 16]), gap3[:, t, lo:hi], ADD
+                )
+            excess = tile("excess%d" % t, [S], F32)
+            nc.scalar.activation(out=excess[:], in_=gap4[:, t, :], func=RELU, scale=-1.0)
+            turned_bank = psum.tile([P, S], F32, name="turned_bank%d" % t, tag="y_bank%d" % (t + 1))
+            for c in range(0, S, P):
+                terms = (h[t][:, c : c + P], gap3[:, t, c : c + P], excess[:, c : c + P])
+                for n, term in enumerate(terms):
+                    nc.tensor.matmul(
+                        turned_bank[:, c : c + P], term, identity[:], start=n == 0, stop=n == len(terms) - 1, is_transpose=True
+                    )
+            turned = tile("turned%d" % t, [S], F32)
+            nc.scalar.copy(out=turned[:], in_=turned_bank[:])
+            result_bank = psum.tile([P, S], F32, name="result_bank%d" % t, tag="y_bank%d" % (3 * (1 - t)))
+            for c in range(0, S, P):
+                nc.tensor.transpose(result_bank[:, c : c + P], turned[:, c : c + P], identity[:])
+            nc.scalar.copy(out=result[:, t, :], in_=result_bank[:])
+            nc.sync.dma_start(out_rows[:, t, :], result[:, t, :])
         gap(gap3, n3_t, 2, 0, S)
-        larger(slice(0, 2), 0, S)
         gap(gap4, n4_t, 2, 0, S)
         (a0, a1), (b0, b1), (c0, c1) = LAST_PARTS
         gap(gap3, n3_t, 3, a0, a1)

@@ -214,7 +214,7 @@ def tile_picked_densegapunder_none_po_kernel(
                 in_=out_bf[:].rearrange("p c t -> p (c t)"),
             )
 
-        for t in (0, 1):
+        def pick(t):
             for lo, hi in HALVES:
                 nc.vector.tensor_scalar(
                     gap3[:, t, lo:hi], windows[t][:].indirect(n3_t[:, lo // 16 : hi // 16]), -1.0, 0.0, MULTIPLY, ADD
@@ -223,22 +223,39 @@ def tile_picked_densegapunder_none_po_kernel(
                 nc.vector.tensor_tensor(
                     gap4[:, t, lo:hi], windows[t][:].indirect(n4_t[:, lo // 16 : hi // 16]), gap3[:, t, lo:hi], ADD
                 )
-            excess = tile("excess%d" % t, [S], F32)
-            nc.scalar.activation(out=excess[:], in_=gap4[:, t, :], func=RELU, scale=-1.0)
-            turned_bank = psum.tile([P, S], F32, name="turned_bank%d" % t, tag="y_bank%d" % (t + 1))
-            for c in range(0, S, P):
-                terms = (h[t][:, c : c + P], gap3[:, t, c : c + P], excess[:, c : c + P])
+
+        def sum_turned(t, half):
+            lo, hi = HALVES[half]
+            unit = 2 * t + half
+            excess = tile("excess%d" % unit, [hi - lo], F32)
+            nc.scalar.activation(out=excess[:], in_=gap4[:, t, lo:hi], func=RELU, scale=-1.0)
+            bank = psum.tile([P, hi - lo], F32, name="turned_bank%d" % unit, tag="y_bank%d" % unit)
+            for c in range(0, hi - lo, P):
+                terms = (h[t][:, lo + c : lo + c + P], gap3[:, t, lo + c : lo + c + P], excess[:, c : c + P])
                 for n, term in enumerate(terms):
-                    nc.tensor.matmul(
-                        turned_bank[:, c : c + P], term, identity[:], start=n == 0, stop=n == len(terms) - 1, is_transpose=True
-                    )
-            turned = tile("turned%d" % t, [S], F32)
-            nc.scalar.copy(out=turned[:], in_=turned_bank[:])
-            result_bank = psum.tile([P, S], F32, name="result_bank%d" % t, tag="y_bank%d" % (3 * (1 - t)))
-            for c in range(0, S, P):
-                nc.tensor.transpose(result_bank[:, c : c + P], turned[:, c : c + P], identity[:])
-            nc.scalar.copy(out=result[:, t, :], in_=result_bank[:])
-            nc.sync.dma_start(out_rows[:, t, :], result[:, t, :])
+                    nc.tensor.matmul(bank[:, c : c + P], term, identity[:], start=n == 0, stop=n == len(terms) - 1, is_transpose=True)
+            turned = tile("turned%d" % unit, [hi - lo], F32)
+            nc.scalar.copy(out=turned[:], in_=bank[:])
+            return turned
+
+        def turn_back(t, half, turned):
+            lo, hi = HALVES[half]
+            unit = 2 * t + half
+            bank = psum.tile([P, hi - lo], F32, name="result_bank%d" % unit, tag="h_bank%d" % unit)
+            for c in range(0, hi - lo, P):
+                nc.tensor.transpose(bank[:, c : c + P], turned[:, c : c + P], identity[:])
+            nc.scalar.copy(out=result[:, t, lo:hi], in_=bank[:])
+
+        pick(0)
+        pick(1)
+        units = ((0, 0), (0, 1), (1, 0), (1, 1))
+        turned_units = []
+        for n, (t, half) in enumerate(units):
+            turned_units.append(sum_turned(t, half))
+            if n > 0:
+                turn_back(units[n - 1][0], units[n - 1][1], turned_units[n - 1])
+        turn_back(units[-1][0], units[-1][1], turned_units[-1])
+        nc.sync.dma_start(out_rows[:, 0:2, :], result[:, 0:2, :])
         gap(gap3, n3_t, 2, 0, S)
         gap(gap4, n4_t, 2, 0, S)
         (a0, a1), (b0, b1), (c0, c1) = LAST_PARTS

from contextlib import ExitStack

import concourse.mybir as mybir
from concourse.masks import make_identity

F32 = mybir.dt.float32
BF16 = mybir.dt.bfloat16
I32 = mybir.dt.int32
U32 = mybir.dt.uint32
U16 = mybir.dt.uint16
U8 = mybir.dt.uint8
FP8X4 = mybir.dt.float8_e4m3fn_x4
FP4X4 = mybir.dt.float4_e2m1fn_x4
COPY = mybir.ActivationFunctionType.Copy
RELU = mybir.ActivationFunctionType.Relu
MULTIPLY = mybir.AluOpType.mult
SUBTRACT = mybir.AluOpType.subtract
ADD = mybir.AluOpType.add
MAXIMUM = mybir.AluOpType.max

P = 128
PACK = 4
TABLE = 2048
S = 512
FLOPS = 2 * 2 * 512 * 512 * 512

HALVES = ((0, 256), (256, 512))
LAST_PARTS = ((0, 256), (256, 384), (384, 512))


def interleave(copy, dst, src):
    copy(
        out=dst.rearrange("p (c i) t -> p c t i", i=PACK),
        in_=src.rearrange("p t (c i) -> p c t i", i=PACK),
    )


def tile_picked_densegapunder_none_po_kernel(
    tc, x_words, x_scales, w1_words, w1_scales, gs, d_words, d_scales, offs, n1, n2, k1, n3, n4, out_0, out_1, out_2
):
    nc = tc.nc
    with ExitStack() as ctx:
        lists = ctx.enter_context(tc.tile_pool(name="lists", bufs=1))
        sb = ctx.enter_context(tc.tile_pool(name="sb", bufs=1))
        psum = ctx.enter_context(tc.psum_pool(name="psum", bufs=1))

        def list_tile(name):
            return lists.tile([P, S // 16], U16, name=name)

        def tile(name, shape, dtype):
            return sb.tile([P] + shape, dtype, name=name, tag=name, align_bytes=64)

        offs_t, k1_t = list_tile("offs_t"), list_tile("k1_t")
        n1_t, n2_t, n3_t, n4_t = list_tile("n1_t"), list_tile("n2_t"), list_tile("n3_t"), list_tile("n4_t")

        x_table = tile("x_table", [TABLE], I32)
        xs_table = tile("xs_table", [TABLE], U8)
        ds_table = tile("ds_table", [TABLE], U8)
        w1_raw = tile("w1_raw", [2 * S], U8)
        w1s_raw = tile("w1s_raw", [S], U8)
        gain = tile("gain", [PACK], F32)
        d_plane = tile("d_plane", [S], U8)

        nc.vector.memset(xs_table[:].bitcast(I32), 0)
        nc.vector.memset(w1s_raw[:].bitcast(I32), 0)
        nc.vector.memset(ds_table[:].bitcast(I32), 0)
        nc.vector.memset(d_plane[:].bitcast(I32), 0)

        identity = tile("identity", [P], F32)
        make_identity(nc, identity[:])

        queues = (nc.sync, nc.scalar)
        nc.sync.dma_start(w1_raw[:].bitcast(I32), w1_words[0].bitcast(I32))
        nc.sync.dma_start(offs_t[:], offs)
        for q in range(4):
            queues[q % 2].dma_start(xs_table[32 * q : 32 * q + 4, :].bitcast(I32), x_scales[0, 4 * q : 4 * q + 4, :].bitcast(I32))
        nc.sync.dma_start(k1_t[:], k1)
        nc.sync.dma_start(x_table[:], x_words[0].rearrange("p n t -> p (n t)").bitcast(I32))
        for q in range(4):
            nc.sync.dma_start(w1s_raw[32 * q : 32 * q + 4, :].bitcast(I32), w1_scales[0, 4 * q : 4 * q + 4, :].bitcast(I32))
        nc.sync.dma_start(ds_table[0:P:8, :].bitcast(I32), d_scales[0].bitcast(I32))
        nc.sync.dma_start(gain[:], gs.rearrange("(p t) o -> p (t o)", t=PACK))
        nc.sync.dma_start(n2_t[:], n2)
        nc.sync.dma_start(n1_t[:], n1)
        nc.sync.dma_start(n3_t[:], n3)
        nc.sync.dma_start(n4_t[:], n4)

        w1_codes = tile("w1_codes", [2 * S], U8)
        nc.vector.tensor_copy(
            out=w1_codes[:].rearrange("p (t m b) -> p t m b", t=PACK, b=2),
            in_=w1_raw[:].rearrange("p (m t b) -> p t m b", t=PACK, b=2),
        )
        d_table = sb.tile([P, TABLE], I32, name="d_table", tag="w1_raw", align_bytes=64)
        nc.sync.dma_start(d_table[:], d_words[0].rearrange("p n t -> p (n t)").bitcast(I32))
        x_plane = tile("x_plane", [S], U8)
        nc.vector.tensor_copy(x_plane[:], xs_table[:].indirect(offs_t[:]))
        x_codes = tile("x_codes", [S], U32)
        nc.vector.tensor_copy(x_codes[:], x_table[:].bitcast(U32).indirect(offs_t[:]))
        w1_plane = tile("w1_plane", [S], U8)
        nc.vector.tensor_copy(
            out=w1_plane[:].rearrange("p (t m) -> p t m", t=PACK),
            in_=w1s_raw[:].rearrange("p (m t) -> p t m", t=PACK),
        )

        y = []
        for t in range(PACK):
            y_bank = psum.tile([P, S], F32, name="y_bank%d" % t, tag="y_bank%d" % t)
            nc.tensor.matmul_mx(
                out=y_bank[:],
                lhsT=w1_codes[:, 2 * P * t : 2 * P * (t + 1)].bitcast(FP4X4),
                lhsT_scale=w1_plane[:, P * t : P * (t + 1)],
                rhs=x_codes[:].bitcast(FP8X4),
                rhs_scale=x_plane[:],
                start=True,
                stop=True,
            )
            y_t = tile("y%d" % t, [S], F32)
            nc.scalar.activation(out=y_t[:], in_=y_bank[:], func=COPY, scale=gain[:, t : t + 1])
            y.append(y_t)

        ds_picked = tile("ds_picked", [S], U8)
        nc.vector.tensor_copy(ds_picked[:], ds_table[:].indirect(k1_t[:]))
        ds_dealt = tile("ds_dealt", [S], U8)
        nc.vector.tensor_copy(
            out=ds_dealt[:].rearrange("p (t m) -> p t m", t=PACK),
            in_=ds_picked[:].rearrange("p (m t) -> p t m", t=PACK),
        )
        for q in range(4):
            nc.sync.dma_start(d_plane[32 * q : 32 * q + 4, :].bitcast(I32), ds_dealt[32 * q : 32 * q + 32 : 8, :].bitcast(I32))

        z = [tile("z_%d" % lo, [PACK, hi - lo], F32) for lo, hi in HALVES]

        def difference(units):
            picked = []
            for t, half in units:
                lo, hi = HALVES[half]
                y_n2 = tile("y_n2_%d_%d" % (t, half), [hi - lo], F32)
                nc.vector.tensor_copy(y_n2[:], y[t][:].indirect(n2_t[:, lo // 16 : hi // 16]))
                picked.append(y_n2)
            for (t, half), y_n2 in zip(units, picked):
                lo, hi = HALVES[half]
                nc.vector.tensor_tensor(z[half][:, t, :], y[t][:].indirect(n1_t[:, lo // 16 : hi // 16]), y_n2[:], SUBTRACT)

        difference(((0, 0), (0, 1)))
        difference(((1, 0), (1, 1)))
        z_rounded = []
        for half, (lo, hi) in enumerate(HALVES):
            difference(((2, half), (3, half)))
            z_bf = tile("z_rounded_%d" % lo, [hi - lo, PACK], BF16)
            interleave(nc.scalar.copy, z_bf[:], z[half][:])
            z_rounded.append(z_bf)

        d_picked = sb.tile([P, S], U32, name="d_picked", tag="y_n2_2_1", align_bytes=64)
        nc.vector.tensor_copy(d_picked[:], d_table[:].bitcast(U32).indirect(k1_t[:]))
        z_codes = tile("z_codes", [S], U32)
        z_plane = tile("z_plane", [S], U8)
        picked_by_row = d_picked[:].bitcast(I32).rearrange("p (m t) -> p m t", t=PACK)
        d_first = tile("d_first", [P], I32)
        for (lo, hi), z_bf in zip(HALVES, z_rounded):
            if hi == S:
                nc.vector.tensor_copy(out=d_first[:], in_=picked_by_row[:, :, 0])
            nc.vector.quantize_mx(
                out=z_codes[:, lo:hi].bitcast(FP8X4), scales=z_plane[:, lo:hi], in_=z_bf[:].rearrange("p c t -> p (c t)")
            )

        d_rest = sb.tile([P, PACK - 1, P], I32, name="d_rest", tag="z_rounded_%d" % HALVES[1][0], align_bytes=64)
        nc.vector.tensor_copy(out=d_rest[:].rearrange("p t m -> p m t"), in_=picked_by_row[:, :, 1:])
        d_codes = [d_first[:]] + [d_rest[:, t, :] for t in range(PACK - 1)]

        windows = [tile("window%d" % t, [2 * S if t == 2 else S], F32) for t in range(PACK)]
        h_2 = tile("h_2", [S], F32)
        h = [windows[0][:], windows[1][:], h_2[:], windows[2][:, S:]]
        for t in range(PACK):
            for lo, hi in HALVES if t == 0 else ((0, S),):
                tag = "y_bank0" if hi < S else "h_bank%d" % t
                h_bank = psum.tile([P, S], F32, name="h_bank%d_%d" % (t, lo), tag=tag)
                nc.tensor.matmul_mx(
                    out=h_bank[:, lo:hi],
                    lhsT=d_codes[t].bitcast(FP8X4),
                    lhsT_scale=d_plane[:, P * t : P * (t + 1)],
                    rhs=z_codes[:, lo:hi].bitcast(FP8X4),
                    rhs_scale=z_plane[:, lo:hi],
                    start=True,
                    stop=True,
                )
                if t >= 2:
                    nc.scalar.activation(out=windows[t][:, lo:hi], in_=h_bank[:, lo:hi], func=COPY, scale=-0.0625)
                nc.scalar.activation(out=h[t][:, lo:hi], in_=h_bank[:, lo:hi], func=COPY, scale=0.0625)

        out_rows = out_0.rearrange("(p t) j -> p t j", t=PACK)
        out_words = out_1[0].rearrange("p n t -> p (n t)").bitcast(I32)
        out_codes = tile("out_codes", [S], I32)
        out_plane = tile("out_plane", [S], U8)
        gap3 = tile("gap3", [PACK, S], F32)
        gap4 = tile("gap4", [PACK, S], F32)
        result = tile("result", [PACK, S], F32)

        def gap(dst, entries, t, lo, hi):
            nc.vector.tensor_tensor(dst[:, t, lo:hi], windows[t][:].indirect(entries[:, lo // 16 : hi // 16]), h[t][:, lo:hi], ADD)

        def larger(rows, lo, hi):
            nc.vector.tensor_tensor(result[:, rows, lo:hi], gap3[:, rows, lo:hi], gap4[:, rows, lo:hi], MAXIMUM)
            nc.sync.dma_start(out_rows[:, rows, lo:hi], result[:, rows, lo:hi])

        def rounded(copy, lo, hi):
            out_bf = tile("out_bf_%d" % lo, [hi - lo, PACK], BF16)
            interleave(copy, out_bf[:], result[:, :, lo:hi])
            return out_bf

        def quantize(out_bf, lo, hi):
            nc.vector.quantize_mx(
                out=out_codes[:, lo:hi].bitcast(FP8X4),
                scales=out_plane[:, lo:hi],
                in_=out_bf[:].rearrange("p c t -> p (c t)"),
            )

        def pick(t):
            for lo, hi in HALVES:
                nc.vector.tensor_scalar(
                    gap3[:, t, lo:hi], windows[t][:].indirect(n3_t[:, lo // 16 : hi // 16]), -1.0, 0.0, MULTIPLY, ADD
                )
            for lo, hi in HALVES:
                nc.vector.tensor_tensor(
                    gap4[:, t, lo:hi], windows[t][:].indirect(n4_t[:, lo // 16 : hi // 16]), gap3[:, t, lo:hi], ADD
                )

        def sum_turned(t, half):
            lo, hi = HALVES[half]
            unit = 2 * t + half
            excess = tile("excess%d" % unit, [hi - lo], F32)
            nc.scalar.activation(out=excess[:], in_=gap4[:, t, lo:hi], func=RELU, scale=-1.0)
            bank = psum.tile([P, hi - lo], F32, name="turned_bank%d" % unit, tag="y_bank%d" % unit)
            for c in range(0, hi - lo, P):
                terms = (h[t][:, lo + c : lo + c + P], gap3[:, t, lo + c : lo + c + P], excess[:, c : c + P])
                for n, term in enumerate(terms):
                    nc.tensor.matmul(bank[:, c : c + P], term, identity[:], start=n == 0, stop=n == len(terms) - 1, is_transpose=True)
            turned = tile("turned%d" % unit, [hi - lo], F32)
            nc.scalar.copy(out=turned[:], in_=bank[:])
            return turned

        def turn_back(t, half, turned):
            lo, hi = HALVES[half]
            unit = 2 * t + half
            bank = psum.tile([P, hi - lo], F32, name="result_bank%d" % unit, tag="h_bank%d" % unit)
            for c in range(0, hi - lo, P):
                nc.tensor.transpose(bank[:, c : c + P], turned[:, c : c + P], identity[:])
            nc.scalar.copy(out=result[:, t, lo:hi], in_=bank[:])

        pick(0)
        pick(1)
        units = ((0, 0), (0, 1), (1, 0), (1, 1))
        turned_units = []
        for n, (t, half) in enumerate(units):
            turned_units.append(sum_turned(t, half))
            if n > 0:
                turn_back(units[n - 1][0], units[n - 1][1], turned_units[n - 1])
        turn_back(units[-1][0], units[-1][1], turned_units[-1])
        nc.sync.dma_start(out_rows[:, 0:2, :], result[:, 0:2, :])
        gap(gap3, n3_t, 2, 0, S)
        gap(gap4, n4_t, 2, 0, S)
        (a0, a1), (b0, b1), (c0, c1) = LAST_PARTS
        gap(gap3, n3_t, 3, a0, a1)
        larger(slice(2, 3), 0, S)
        gap(gap4, n4_t, 3, a0, a1)
        gap(gap3, n3_t, 3, b0, b1)
        larger(slice(3, 4), a0, a1)
        out_a = rounded(nc.scalar.copy, a0, a1)
        gap(gap4, n4_t, 3, b0, b1)
        gap(gap3, n3_t, 3, c0, c1)
        larger(slice(3, 4), b0, b1)
        out_b = rounded(nc.scalar.copy, b0, b1)
        gap(gap4, n4_t, 3, c0, c1)
        quantize(out_a, a0, a1)
        nc.sync.dma_start(out_words[:, a0:a1], out_codes[:, a0:a1])
        larger(slice(3, 4), c0, c1)
        out_c = rounded(nc.vector.tensor_copy, c0, c1)
        quantize(out_b, b0, b1)
        quantize(out_c, c0, c1)
        nc.sync.dma_start(out_words[:, b0:c1], out_codes[:, b0:c1])
        for q in range(4):
            queues[1 - q % 2].dma_start(out_2[0, 4 * q : 4 * q + 4, :].bitcast(I32), out_plane[32 * q : 32 * q + 4, :].bitcast(I32))
